import numpy as np
import ml_dtypes


def mxq(x, axis, fmt="e4m3"):
    dtype, down = {"e4m3": (ml_dtypes.float8_e4m3fn, 7), "e5m2": (ml_dtypes.float8_e5m2, 14)}[fmt]
    v = np.moveaxis(np.asarray(x, np.float32).astype(ml_dtypes.bfloat16).astype(np.float64), axis, -1)
    blocks = v.reshape(v.shape[:-1] + (-1, 32))
    amax = np.abs(blocks).max(-1, keepdims=True)
    byte = np.maximum(np.where(amax > 0, np.frexp(amax)[1] - 1 + 127, 0) - down, 1)
    scale = np.exp2(byte - 127.0)
    codes = (blocks / scale).astype(np.float32).astype(dtype).astype(np.float64)
    return np.moveaxis((codes * scale).reshape(v.shape), -1, axis)


WIDE = False


def mx_kscale(k):
    if not WIDE:
        return np.ones(k)
    levels = np.array([10, -10, 5, -5, 0])
    if k % 512:
        return np.exp2(np.random.permutation(np.resize(levels, k // 32))).repeat(32)
    a = np.empty((k // 512, 16))
    for p in range(k // 512):
        a[p, :8] = np.random.permutation(np.resize(levels, 8))
        for g in range(8):
            far = levels[np.abs(levels - a[p, g]) >= 10]
            a[p, g + 8] = far[np.random.randint(len(far))]
    return np.exp2(a.ravel()).repeat(32)


def f64(x):
    return np.asarray(x).astype(np.float64)


def striped(idx):
    return np.tile(idx.reshape(-1, 16).T, (8, 1)).astype(np.uint16)


def unstriped(offs):
    return offs[:16].T.reshape(-1).astype(np.int64)


def striped8(idx):
    return np.concatenate([x.reshape(-1, 16).T for x in idx]).astype(np.uint16)


def runs(offs, k):
    lists = np.stack([offs[16 * r : 16 * r + 16].T.reshape(-1) for r in range(8)]).astype(np.int64)
    return lists[np.arange(k) % 512 // 64]


def pack_weight(w):
    k, n = w.shape
    w = f64(np.asarray(w, np.float32).astype(ml_dtypes.bfloat16)).reshape(k // 32, 32, n)
    amax = np.abs(w).max(1)
    byte = np.clip(np.where(amax > 0, np.frexp(amax)[1] - 1 + 127 - 7, 1), 1, 254)
    scaled = (w * np.exp2(127.0 - byte)[:, None, :]).reshape(k, n).astype(np.float32)
    words = np.ascontiguousarray(scaled.reshape(k // 512, 128, 4, n).transpose(0, 1, 3, 2)).astype(ml_dtypes.float8_e4m3fn).view(np.uint8)
    return words, np.ascontiguousarray(byte.astype(np.uint8).reshape(k // 512, 16, n))


def unpack_weight(words, scales):
    g, p, n, _ = words.shape
    vals = np.ascontiguousarray(words).view(ml_dtypes.float8_e4m3fn).astype(np.float64) * np.repeat(np.exp2(scales.astype(np.float64) - 127.0), 8, axis=1)[..., None]
    return vals.transpose(0, 1, 3, 2).reshape(g * 512, n)


E2M1 = np.array([0.0, 0.5, 1.0, 1.5, 2.0, 3.0, 4.0, 6.0, -0.0, -0.5, -1.0, -1.5, -2.0, -3.0, -4.0, -6.0])


def pack_fp4(w):
    k, n = w.shape
    w = f64(np.asarray(w, np.float32).astype(ml_dtypes.bfloat16)).reshape(k // 32, 32, n)
    amax = np.abs(w).max(1)
    mant, ex = np.frexp(amax / 6.0)
    byte = np.clip(np.where(amax > 0, np.where(mant > 0.5, ex, ex - 1) + 127, 1), 1, 254)
    scaled = (w * np.exp2(127.0 - byte)[:, None, :]).reshape(k, n).astype(np.float32)
    c = np.ascontiguousarray(scaled.reshape(k // 512, 128, 4, n).transpose(0, 1, 3, 2)).astype(ml_dtypes.float4_e2m1fn).view(np.uint8) & 0xF
    words = (c[..., 0::2] | (c[..., 1::2] << 4)).reshape(k // 512, 128, 2 * n)
    return np.ascontiguousarray(words), np.ascontiguousarray(byte.astype(np.uint8).reshape(k // 512, 16, n))


def unpack_fp4(words, scales):
    g, _, n = scales.shape
    words = np.ascontiguousarray(words).reshape(g, 128, n, 2)
    nib = np.empty((g, 128, n, 4), np.uint8)
    nib[..., 0::2] = words & 0xF
    nib[..., 1::2] = words >> 4
    vals = E2M1[nib] * np.repeat(np.exp2(scales.astype(np.float64) - 127.0), 8, axis=1)[..., None]
    return vals.transpose(0, 1, 3, 2).reshape(g * 512, n)


def sigmoid(v):
    return 1.0 / (1.0 + np.exp(-np.maximum(v, -700.0)))

def planes(y):
    n, m = y.shape
    v = y.astype(np.float32).astype(ml_dtypes.bfloat16).astype(np.float64).reshape(n // 32, 32, m)
    top = np.abs(v).max(1)
    byte = np.clip(np.where(top > 0, np.frexp(top)[1] - 1 + 127 - 7, 1), 1, 254)
    codes = (v * np.exp2(127.0 - byte)[:, None, :]).reshape(n, m).astype(np.float32).astype(ml_dtypes.float8_e4m3fn).view(np.uint8)
    words = codes.reshape(n // 512, 128, 4, m).transpose(0, 1, 3, 2)
    return np.ascontiguousarray(words), np.ascontiguousarray(byte.astype(np.uint8).reshape(n // 512, 16, m))


K, T, S, H, C = 512, 2048, 512, 512, 512


def setup_inputs():
    n = np.random.standard_normal
    s = mx_kscale(K)[:, None]
    packed_xT = pack_weight(n((K, T)) * s)
    packed_w1 = pack_fp4(n((K, H)) / np.sqrt(K) / s)
    return {
        "x_words": packed_xT[0],
        "x_scales": packed_xT[1],
        "w1_words": packed_w1[0],
        "w1_scales": packed_w1[1],
        "gs": (np.random.uniform(0.5, 1.5, (K, 1)) / s).astype(np.float32),
        "offs": striped(np.random.permutation(T)[:S]),
        "n1": striped8(np.stack([np.random.permutation(S) for _ in range(8)])),
        "ca": striped(np.random.permutation(T)[:C]),
        "cb": striped(np.random.permutation(T)[:C]),
        "n2": striped8(np.stack([np.random.permutation(S) for _ in range(8)])),
        "n3": striped8(np.stack([np.random.permutation(S) for _ in range(8)])),
    }


def reference(x_words, x_scales, w1_words, w1_scales, gs, offs, n1, ca, cb, n2, n3):
    x_ca = unpack_weight(x_words, x_scales)[:, unstriped(ca)]
    xq = unpack_weight(x_words, x_scales)[:, unstriped(offs)]
    y = unpack_fp4(w1_words, w1_scales).T @ xq
    st = y * (sigmoid(y[np.arange(H)[:, None], runs(n1, H)]))
    z = f64(gs) * (np.maximum(st, st[np.arange(H)[:, None], runs(n1, H)]))
    zq = mxq(z, 0, "e4m3")
    a = 0.0625 * (x_ca.T @ zq)
    x_cb = unpack_weight(x_words, x_scales)[:, unstriped(cb)]
    b = 0.0625 * (x_cb.T @ zq)
    out_0 = np.maximum(a, b[np.arange(C)[:, None], runs(n3, C)]) - (np.minimum(a[np.arange(C)[:, None], runs(n2, C)], b))
    return (out_0,) + planes(out_0)

@@ -1,0 +1,219 @@
+from contextlib import ExitStack
+
+import concourse.mybir as mybir
+
+K, T, S, H, C = 512, 2048, 512, 512, 512
+FLOPS = 3 * 2 * 512 * 512 * 512
+
+F32 = mybir.dt.float32
+BF16 = mybir.dt.bfloat16
+I32 = mybir.dt.int32
+U32 = mybir.dt.uint32
+U16 = mybir.dt.uint16
+U8 = mybir.dt.uint8
+FP8X4 = mybir.dt.float8_e4m3fn_x4
+FP4X4 = mybir.dt.float4_e2m1fn_x4
+ACT = mybir.ActivationFunctionType
+ALU = mybir.AluOpType
+
+P = 128
+PACK = 4
+HALF = 256
+LIST_COLS = HALF // 16
+SIXTEENTH = 0.0625
+
+
+def tile_picked_ccmpmaxbtwicp_none_po_kernel(
+    tc, x_words, x_scales, w1_words, w1_scales, gs, offs, n1, ca, cb, n2, n3, out_0, out_1, out_2
+):
+    nc = tc.nc
+    with ExitStack() as ctx:
+        keep = ctx.enter_context(tc.tile_pool(name="keep", bufs=1))
+        psum = ctx.enter_context(tc.psum_pool(name="psum", bufs=1))
+
+        def sb(name, shape, dtype, tag=None):
+            return keep.tile(shape, dtype, name=name, tag=tag or name, align_bytes=64)
+
+        def load_list(name, src):
+            lst = keep.tile([P, S // 16], U16, name=name)
+            nc.sync.dma_start(lst[:], src)
+            return lst
+
+        def half_of(lst, h):
+            return lst[:, h * LIST_COLS : (h + 1) * LIST_COLS]
+
+        def cols(h):
+            return slice(h * HALF, (h + 1) * HALF)
+
+        xs = sb("xs", [P, T], U8)
+        ws = sb("ws", [P, H], U8)
+        nc.gpsimd.memset(xs[:].bitcast(I32), 0)
+        nc.vector.memset(ws[:].bitcast(I32), 0)
+        for q in range(4):
+            nc.sync.dma_start(xs[32 * q : 32 * q + 4, :].bitcast(I32), x_scales[0, 4 * q : 4 * q + 4, :].bitcast(I32))
+        for q in range(4):
+            nc.gpsimd.dma_start(ws[32 * q : 32 * q + 4, :].bitcast(I32), w1_scales[0, 4 * q : 4 * q + 4, :].bitcast(I32))
+        offs_l = load_list("offs_l", offs)
+        ww = sb("ww", [P, 2 * H], U8)
+        nc.sync.dma_start(ww[:].bitcast(I32), w1_words[0].bitcast(I32))
+        xw = sb("xw", [P, T], U32)
+        nc.sync.dma_start(xw[:].bitcast(I32), x_words[0].rearrange("p n t -> p (n t)").bitcast(I32))
+        ca_l = load_list("ca_l", ca)
+        n1_l = load_list("n1_l", n1)
+        cb_l = load_list("cb_l", cb)
+        gain = sb("gain", [P, PACK], F32)
+        nc.sync.dma_start(gain[:], gs.rearrange("(p t) o -> p (t o)", t=PACK))
+        n2_l = load_list("n2_l", n2)
+        n3_l = load_list("n3_l", n3)
+
+        def pick_scales(name, lst, tag=None):
+            picked = sb(name, [P, S], U8, tag)
+            nc.vector.tensor_copy(picked[:], xs[:].indirect(lst[:]))
+            return picked
+
+        def deal_scales(name, src):
+            dealt = sb(name, [P, S], U8)
+            nc.vector.tensor_copy(
+                dealt[:].rearrange("p (t m) -> p m t", t=PACK), src[:].rearrange("p (m t) -> p m t", t=PACK)
+            )
+            return dealt
+
+        def pick_words_dealt(name, lst, tag=None):
+            dealt = sb(name, [P, S], U32, tag)
+            nc.vector.tensor_copy(dealt[:].rearrange("p (t m) -> p m t", t=PACK), xw[:].indirect(lst[:]))
+            return dealt
+
+        q_scales = pick_scales("q_scales", offs_l)
+        w_words = sb("w_words", [P, 2 * H], U8)
+        nc.vector.tensor_copy(
+            w_words[:].rearrange("p (t m b) -> p m t b", t=PACK, b=2),
+            ww[:].rearrange("p (m t b) -> p m t b", t=PACK, b=2),
+        )
+        w_scales = deal_scales("w_scales", ws)
+        q_words = sb("q_words", [P, S], U32)
+        nc.vector.tensor_copy(q_words[:], xw[:].indirect(offs_l[:]))
+
+        a_scales = deal_scales("a_scales", pick_scales("a_raw", ca_l, "ws"))
+        a_words = pick_words_dealt("a_words", ca_l, "ww")
+
+        y = []
+        sig = []
+        for t in range(PACK):
+            acc = psum.tile([P, S], F32, name=f"y_acc{t}", tag=f"bank{t}")
+            nc.tensor.matmul_mx(
+                out=acc[:],
+                lhsT=w_words[:, 2 * P * t : 2 * P * (t + 1)].bitcast(FP4X4),
+                lhsT_scale=w_scales[:, P * t : P * (t + 1)],
+                rhs=q_words[:].bitcast(FP8X4),
+                rhs_scale=q_scales[:],
+                start=True,
+                stop=True,
+            )
+            y.append(sb(f"y{t}", [P, S], F32))
+            nc.scalar.copy(y[t][:], acc[:])
+            sig.append(sb(f"sig{t}", [P, S], F32))
+            for h in range(2):
+                nc.scalar.activation(sig[t][:, cols(h)], y[t][:].indirect(half_of(n1_l, h)), ACT.Sigmoid)
+
+        st = [sb(f"st{t}", [P, S], F32) for t in range(PACK)]
+        z_planes = [sb(f"z_planes{h}", [P, PACK, HALF], BF16) for h in range(2)]
+        z_words = [sb(f"z_words{h}", [P, HALF], U32) for h in range(2)]
+        z_scales = [sb(f"z_scales{h}", [P, HALF], U8) for h in range(2)]
+
+        def gate(t):
+            nc.vector.tensor_tensor(st[t][:], y[t][:], sig[t][:], ALU.mult)
+
+        fetched = {}
+
+        def fetch_st(t, h):
+            fetched[t, h] = sb(f"st_far{t}{h}", [P, HALF], F32)
+            nc.vector.tensor_copy(fetched[t, h][:], st[t][:].indirect(half_of(n1_l, h)))
+
+        def larger(t, h):
+            big = sb(f"big{t}{h}", [P, HALF], F32)
+            nc.vector.tensor_tensor(big[:], st[t][:, cols(h)], fetched[t, h][:], ALU.max)
+            nc.scalar.activation(z_planes[h][:, t, :], big[:], ACT.Copy, scale=gain[:, t : t + 1])
+
+        def weave(dst, src):
+            return (
+                dst[:].rearrange("p (c i t) -> p c t i", i=4, t=PACK),
+                src[:].rearrange("p t (c i) -> p c t i", i=4),
+            )
+
+        for t in range(PACK):
+            gate(t)
+            for h in range(2):
+                fetch_st(t, h)
+            for h in range(2):
+                larger(t, h)
+        b_raw = pick_scales("b_raw", cb_l, "st_far31")
+        z_woven = [sb(f"z_woven{h}", [P, PACK * HALF], BF16) for h in range(2)]
+        for h in range(2):
+            nc.vector.tensor_copy(*weave(z_woven[h], z_planes[h]))
+        nc.vector.quantize_mx(out=z_words[0][:].bitcast(FP8X4), scales=z_scales[0][:], in_=z_woven[0][:])
+        b_scales = deal_scales("b_scales", b_raw)
+        nc.vector.quantize_mx(out=z_words[1][:].bitcast(FP8X4), scales=z_scales[1][:], in_=z_woven[1][:])
+        b_words = pick_words_dealt("b_words", cb_l, "z_woven1")
+
+        a = [sb(f"a{t}", [P, S], F32) for t in range(PACK)]
+        b = [sb(f"b{t}", [P, S], F32) for t in range(PACK)]
+        a_acc = {}
+        b_acc = {}
+        for h in range(2):
+            for u in range(2):
+                a_acc[h, u] = psum.tile([P, 2, HALF], F32, name=f"a_acc{h}{u}", tag=f"bank{4 + 2 * h + u}")
+                b_acc[h, u] = psum.tile([P, 2, HALF], F32, name=f"b_acc{h}{u}", tag=f"bank{2 * h + u}")
+
+        def score(acc, words, scales, dst, h, u):
+            for t in range(2 * u, 2 * u + 2):
+                nc.tensor.matmul_mx(
+                    out=acc[h, u][:, t % 2, :],
+                    lhsT=words[:, P * t : P * (t + 1)].bitcast(FP8X4),
+                    lhsT_scale=scales[:, P * t : P * (t + 1)],
+                    rhs=z_words[h][:].bitcast(FP8X4),
+                    rhs_scale=z_scales[h][:],
+                    start=True,
+                    stop=True,
+                )
+            for t in range(2 * u, 2 * u + 2):
+                nc.scalar.activation(dst[t][:, cols(h)], acc[h, u][:, t % 2, :], ACT.Copy, scale=SIXTEENTH)
+
+        for h in range(2):
+            for u in range(2):
+                score(a_acc, a_words, a_scales, a, h, u)
+        for u in range(2):
+            for h in range(2):
+                score(b_acc, b_words, b_scales, b, h, u)
+
+        out_rows = out_0.rearrange("(p t) j -> p t j", t=PACK)
+        out_words = out_1[0].rearrange("p n t -> p (n t)").bitcast(I32)
+        o_scales = sb("o_scales", [P, S], U8)
+        for h in range(2):
+            a_far = sb(f"a_far{h}", [P, PACK, HALF], F32)
+            b_far = sb(f"b_far{h}", [P, PACK, HALF], F32)
+            hi = sb(f"hi{h}", [P, PACK, HALF], F32)
+            lo = sb(f"lo{h}", [P, PACK, HALF], F32)
+            res = sb(f"res{h}", [P, PACK, HALF], F32)
+            for u in range(2):
+                pair = slice(2 * u, 2 * u + 2)
+                for t in range(2 * u, 2 * u + 2):
+                    nc.vector.tensor_copy(a_far[:, t, :], a[t][:].indirect(half_of(n2_l, h)))
+                for t in range(2 * u, 2 * u + 2):
+                    nc.vector.tensor_copy(b_far[:, t, :], b[t][:].indirect(half_of(n3_l, h)))
+                nc.vector.scalar_tensor_tensor(lo[:, pair, :], b_acc[h, u][:], SIXTEENTH, a_far[:, pair, :], ALU.mult, ALU.min)
+                nc.vector.scalar_tensor_tensor(hi[:, pair, :], a_acc[h, u][:], SIXTEENTH, b_far[:, pair, :], ALU.mult, ALU.max)
+            for u in range(2):
+                pair = slice(2 * u, 2 * u + 2)
+                nc.vector.tensor_tensor(res[:, pair, :], hi[:, pair, :], lo[:, pair, :], ALU.subtract)
+                nc.sync.dma_start(out_rows[:, pair, cols(h)], res[:, pair, :])
+            woven = sb(f"o_woven{h}", [P, PACK * HALF], BF16)
+            if h == 0:
+                nc.scalar.copy(*weave(woven, res))
+            else:
+                nc.vector.tensor_copy(*weave(woven, res))
+            o_words = sb(f"o_words{h}", [P, HALF], U32)
+            nc.vector.quantize_mx(out=o_words[:].bitcast(FP8X4), scales=o_scales[:, cols(h)], in_=woven[:])
+            nc.sync.dma_start(out_words[:, cols(h)], o_words[:].bitcast(I32))
+        for q in range(4):
+            queue = nc.sync if q % 2 else nc.scalar
+            queue.dma_start(out_2[0, 4 * q : 4 * q + 4, :].bitcast(I32), o_scales[32 * q : 32 * q + 4, :].bitcast(I32))

@@ -47,17 +47,21 @@ def tile_picked_ccmpmaxbtwicp_none_po_kernel(
 
         xs = sb("xs", [P, T], U8)
         ws = sb("ws", [P, H], U8)
+        warm = sb("warm", [P, 8], F32)
         nc.gpsimd.memset(xs[:].bitcast(I32), 0)
-        nc.vector.memset(ws[:].bitcast(I32), 0)
-        for q in range(4):
-            nc.sync.dma_start(xs[32 * q : 32 * q + 4, :].bitcast(I32), x_scales[0, 4 * q : 4 * q + 4, :].bitcast(I32))
-        for q in range(4):
-            nc.gpsimd.dma_start(ws[32 * q : 32 * q + 4, :].bitcast(I32), w1_scales[0, 4 * q : 4 * q + 4, :].bitcast(I32))
+        nc.gpsimd.memset(ws[:].bitcast(I32), 0)
+        nc.vector.memset(warm[:, 0:1], 0.0)
+        nc.scalar.activation(warm[:, 1:2], warm[:, 0:1], ACT.Sigmoid)
         offs_l = load_list("offs_l", offs)
         ww = sb("ww", [P, 2 * H], U8)
         nc.sync.dma_start(ww[:].bitcast(I32), w1_words[0].bitcast(I32))
         xw = sb("xw", [P, T], U32)
         nc.sync.dma_start(xw[:].bitcast(I32), x_words[0].rearrange("p n t -> p (n t)").bitcast(I32))
+        for q in range(4):
+            nc.sync.dma_start(xs[32 * q : 32 * q + 4, :].bitcast(I32), x_scales[0, 4 * q : 4 * q + 4, :].bitcast(I32))
+        for q in range(4):
+            queue = nc.gpsimd if q == 3 else nc.sync
+            queue.dma_start(ws[32 * q : 32 * q + 4, :].bitcast(I32), w1_scales[0, 4 * q : 4 * q + 4, :].bitcast(I32))
         ca_l = load_list("ca_l", ca)
         n1_l = load_list("n1_l", n1)
         cb_l = load_list("cb_l", cb)
@@ -83,15 +87,15 @@ def tile_picked_ccmpmaxbtwicp_none_po_kernel(
             nc.vector.tensor_copy(dealt[:].rearrange("p (t m) -> p m t", t=PACK), xw[:].indirect(lst[:]))
             return dealt
 
-        q_scales = pick_scales("q_scales", offs_l)
         w_words = sb("w_words", [P, 2 * H], U8)
         nc.vector.tensor_copy(
             w_words[:].rearrange("p (t m b) -> p m t b", t=PACK, b=2),
             ww[:].rearrange("p (m t b) -> p m t b", t=PACK, b=2),
         )
-        w_scales = deal_scales("w_scales", ws)
         q_words = sb("q_words", [P, S], U32)
         nc.vector.tensor_copy(q_words[:], xw[:].indirect(offs_l[:]))
+        q_scales = pick_scales("q_scales", offs_l)
+        w_scales = deal_scales("w_scales", ws)
 
         a_scales = deal_scales("a_scales", pick_scales("a_raw", ca_l, "ws"))
         a_words = pick_words_dealt("a_words", ca_l, "ww")
@@ -115,13 +119,15 @@ def tile_picked_ccmpmaxbtwicp_none_po_kernel(
             for h in range(2):
                 nc.scalar.activation(sig[t][:, cols(h)], y[t][:].indirect(half_of(n1_l, h)), ACT.Sigmoid)
 
-        st = [sb(f"st{t}", [P, S], F32) for t in range(PACK)]
+        st = {}
         z_planes = [sb(f"z_planes{h}", [P, PACK, HALF], BF16) for h in range(2)]
         z_words = [sb(f"z_words{h}", [P, HALF], U32) for h in range(2)]
         z_scales = [sb(f"z_scales{h}", [P, HALF], U8) for h in range(2)]
 
         def gate(t):
-            nc.vector.tensor_tensor(st[t][:], y[t][:], sig[t][:], ALU.mult)
+            st[t] = sb(f"st{t}", [P, S], F32, f"st{t % 2}")
+            engine = nc.gpsimd if t else nc.vector
+            engine.tensor_tensor(st[t][:], y[t][:], sig[t][:], ALU.mult)
 
         fetched = {}
 
@@ -148,8 +154,8 @@ def tile_picked_ccmpmaxbtwicp_none_po_kernel(
                 larger(t, h)
         b_raw = pick_scales("b_raw", cb_l, "st_far31")
         z_woven = [sb(f"z_woven{h}", [P, PACK * HALF], BF16) for h in range(2)]
-        for h in range(2):
-            nc.vector.tensor_copy(*weave(z_woven[h], z_planes[h]))
+        nc.scalar.copy(*weave(z_woven[0], z_planes[0]))
+        nc.vector.tensor_copy(*weave(z_woven[1], z_planes[1]))
         nc.vector.quantize_mx(out=z_words[0][:].bitcast(FP8X4), scales=z_scales[0][:], in_=z_woven[0][:])
         b_scales = deal_scales("b_scales", b_raw)
         nc.vector.quantize_mx(out=z_words[1][:].bitcast(FP8X4), scales=z_scales[1][:], in_=z_woven[1][:])
@@ -204,7 +210,8 @@ def tile_picked_ccmpmaxbtwicp_none_po_kernel(
                 nc.vector.scalar_tensor_tensor(hi[:, pair, :], a_acc[h, u][:], SIXTEENTH, b_far[:, pair, :], ALU.mult, ALU.max)
             for u in range(2):
                 pair = slice(2 * u, 2 * u + 2)
-                nc.vector.tensor_tensor(res[:, pair, :], hi[:, pair, :], lo[:, pair, :], ALU.subtract)
+                engine = nc.vector if (h, u) == (1, 1) else nc.gpsimd
+                engine.tensor_tensor(res[:, pair, :], hi[:, pair, :], lo[:, pair, :], ALU.subtract)
                 nc.sync.dma_start(out_rows[:, pair, cols(h)], res[:, pair, :])
             woven = sb(f"o_woven{h}", [P, PACK * HALF], BF16)
             if h == 0:

@@ -56,11 +56,13 @@ def tile_picked_ccmpmaxbtwicp_none_po_kernel(
         ww = sb("ww", [P, 2 * H], U8)
         nc.sync.dma_start(ww[:].bitcast(I32), w1_words[0].bitcast(I32))
         xw = sb("xw", [P, T], U32)
-        nc.sync.dma_start(xw[:].bitcast(I32), x_words[0].rearrange("p n t -> p (n t)").bitcast(I32))
+        x_rows = x_words[0].rearrange("p n t -> p (n t)").bitcast(I32)
+        nc.sync.dma_start(xw[:, : T // 2].bitcast(I32), x_rows[:, : T // 2])
         for q in range(4):
             nc.sync.dma_start(xs[32 * q : 32 * q + 4, :].bitcast(I32), x_scales[0, 4 * q : 4 * q + 4, :].bitcast(I32))
+        nc.sync.dma_start(xw[:, T // 2 :].bitcast(I32), x_rows[:, T // 2 :])
         for q in range(4):
-            queue = nc.gpsimd if q == 3 else nc.sync
+            queue = nc.gpsimd if q >= 2 else nc.sync
             queue.dma_start(ws[32 * q : 32 * q + 4, :].bitcast(I32), w1_scales[0, 4 * q : 4 * q + 4, :].bitcast(I32))
         ca_l = load_list("ca_l", ca)
         n1_l = load_list("n1_l", n1)
@@ -75,8 +77,8 @@ def tile_picked_ccmpmaxbtwicp_none_po_kernel(
             nc.vector.tensor_copy(picked[:], xs[:].indirect(lst[:]))
             return picked
 
-        def deal_scales(name, src):
-            dealt = sb(name, [P, S], U8)
+        def deal_scales(name, src, tag=None):
+            dealt = sb(name, [P, S], U8, tag)
             nc.vector.tensor_copy(
                 dealt[:].rearrange("p (t m) -> p m t", t=PACK), src[:].rearrange("p (m t) -> p m t", t=PACK)
             )
@@ -92,16 +94,20 @@ def tile_picked_ccmpmaxbtwicp_none_po_kernel(
             w_words[:].rearrange("p (t m b) -> p m t b", t=PACK, b=2),
             ww[:].rearrange("p (m t b) -> p m t b", t=PACK, b=2),
         )
+        q_scales = pick_scales("q_scales", offs_l)
         q_words = sb("q_words", [P, S], U32)
         nc.vector.tensor_copy(q_words[:], xw[:].indirect(offs_l[:]))
-        q_scales = pick_scales("q_scales", offs_l)
         w_scales = deal_scales("w_scales", ws)
 
         a_scales = deal_scales("a_scales", pick_scales("a_raw", ca_l, "ws"))
         a_words = pick_words_dealt("a_words", ca_l, "ww")
+        b_raw = pick_scales("b_raw", cb_l, "ws")
 
+        first = slice(0, S)
+        second = slice(S, 2 * S)
         y = []
-        sig = []
+        wide_a = [sb(f"wide_a{t}", [P, 2 * S], F32) for t in range(PACK)]
+        wide_b = [sb(f"wide_b{t}", [P, 2 * S], F32) for t in range(PACK)]
         for t in range(PACK):
             acc = psum.tile([P, S], F32, name=f"y_acc{t}", tag=f"bank{t}")
             nc.tensor.matmul_mx(
@@ -115,112 +121,106 @@ def tile_picked_ccmpmaxbtwicp_none_po_kernel(
             )
             y.append(sb(f"y{t}", [P, S], F32))
             nc.scalar.copy(y[t][:], acc[:])
-            sig.append(sb(f"sig{t}", [P, S], F32))
             for h in range(2):
-                nc.scalar.activation(sig[t][:, cols(h)], y[t][:].indirect(half_of(n1_l, h)), ACT.Sigmoid)
+                nc.scalar.activation(wide_a[t][:, second][:, cols(h)], y[t][:].indirect(half_of(n1_l, h)), ACT.Sigmoid)
 
-        st = {}
-        z_planes = [sb(f"z_planes{h}", [P, PACK, HALF], BF16) for h in range(2)]
-        z_words = [sb(f"z_words{h}", [P, HALF], U32) for h in range(2)]
-        z_scales = [sb(f"z_scales{h}", [P, HALF], U8) for h in range(2)]
+        def pieces(t):
+            if t < PACK - 1:
+                return [slice(0, S)]
+            return [cols(0), cols(1)]
 
-        def gate(t):
-            st[t] = sb(f"st{t}", [P, S], F32, f"st{t % 2}")
-            engine = nc.gpsimd if t else nc.vector
-            engine.tensor_tensor(st[t][:], y[t][:], sig[t][:], ALU.mult)
+        def entries(lst, piece):
+            return lst[:, piece.start // 16 : piece.stop // 16]
 
-        fetched = {}
-
-        def fetch_st(t, h):
-            fetched[t, h] = sb(f"st_far{t}{h}", [P, HALF], F32)
-            nc.vector.tensor_copy(fetched[t, h][:], st[t][:].indirect(half_of(n1_l, h)))
-
-        def larger(t, h):
-            big = sb(f"big{t}{h}", [P, HALF], F32)
-            nc.vector.tensor_tensor(big[:], st[t][:, cols(h)], fetched[t, h][:], ALU.max)
-            nc.scalar.activation(z_planes[h][:, t, :], big[:], ACT.Copy, scale=gain[:, t : t + 1])
-
-        def weave(dst, src):
+        def weave(dst, src, planes):
             return (
-                dst[:].rearrange("p (c i t) -> p c t i", i=4, t=PACK),
-                src[:].rearrange("p t (c i) -> p c t i", i=4),
+                dst[:].rearrange("p (c i t) -> p c t i", i=4, t=PACK)[:, :, planes, :],
+                src.rearrange("p t (c i) -> p c t i", i=4),
             )
 
         for t in range(PACK):
-            gate(t)
+            st = wide_a[t][:, first]
+            far = wide_a[(t + 2) % PACK][:, first]
+            big = wide_b[t][:, second]
+            nc.gpsimd.tensor_tensor(st, y[t][:], wide_a[t][:, second], ALU.mult)
             for h in range(2):
-                fetch_st(t, h)
+                nc.vector.tensor_copy(far[:, cols(h)], wide_a[t][:].indirect(half_of(n1_l, h)))
             for h in range(2):
-                larger(t, h)
-        b_raw = pick_scales("b_raw", cb_l, "st_far31")
-        z_woven = [sb(f"z_woven{h}", [P, PACK * HALF], BF16) for h in range(2)]
-        nc.scalar.copy(*weave(z_woven[0], z_planes[0]))
-        nc.vector.tensor_copy(*weave(z_woven[1], z_planes[1]))
-        nc.vector.quantize_mx(out=z_words[0][:].bitcast(FP8X4), scales=z_scales[0][:], in_=z_woven[0][:])
+                nc.vector.tensor_tensor(big[:, cols(h)], st[:, cols(h)], far[:, cols(h)], ALU.max)
         b_scales = deal_scales("b_scales", b_raw)
-        nc.vector.quantize_mx(out=z_words[1][:].bitcast(FP8X4), scales=z_scales[1][:], in_=z_woven[1][:])
+
+        z_planes = [sb(f"z_planes{h}", [P, PACK, HALF], BF16, f"y{h + 2}") for h in range(2)]
+        z_woven = [sb(f"z_woven{h}", [P, PACK * HALF], BF16) for h in range(2)]
+        for t in range(PACK):
+            for h in range(2):
+                big = wide_b[t][:, second][:, cols(h)]
+                if (t, h) == (PACK - 1, 1):
+                    nc.vector.tensor_scalar(z_planes[h][:, t, :], big, gain[:, t : t + 1], None, ALU.mult)
+                else:
+                    nc.scalar.activation(z_planes[h][:, t, :], big, ACT.Copy, scale=gain[:, t : t + 1])
+        nc.scalar.copy(*weave(z_woven[0], z_planes[0][:], slice(0, PACK)))
+        nc.vector.tensor_copy(*weave(z_woven[1], z_planes[1][:], slice(0, PACK)))
+        z_words = sb("z_words", [P, S], U32)
+        z_scales = sb("z_scales", [P, S], U8)
+        for h in range(2):
+            nc.vector.quantize_mx(out=z_words[:, cols(h)].bitcast(FP8X4), scales=z_scales[:, cols(h)], in_=z_woven[h][:])
         b_words = pick_words_dealt("b_words", cb_l, "z_woven1")
 
-        a = [sb(f"a{t}", [P, S], F32) for t in range(PACK)]
-        b = [sb(f"b{t}", [P, S], F32) for t in range(PACK)]
-        a_acc = {}
-        b_acc = {}
-        for h in range(2):
-            for u in range(2):
-                a_acc[h, u] = psum.tile([P, 2, HALF], F32, name=f"a_acc{h}{u}", tag=f"bank{4 + 2 * h + u}")
-                b_acc[h, u] = psum.tile([P, 2, HALF], F32, name=f"b_acc{h}{u}", tag=f"bank{2 * h + u}")
+        a_acc = [psum.tile([P, S], F32, name=f"a_acc{t}", tag=f"bank{PACK + t}") for t in range(PACK)]
+        b_acc = [psum.tile([P, S], F32, name=f"b_acc{t}", tag=f"bank{t}") for t in range(PACK)]
 
-        def score(acc, words, scales, dst, h, u):
-            for t in range(2 * u, 2 * u + 2):
-                nc.tensor.matmul_mx(
-                    out=acc[h, u][:, t % 2, :],
-                    lhsT=words[:, P * t : P * (t + 1)].bitcast(FP8X4),
-                    lhsT_scale=scales[:, P * t : P * (t + 1)],
-                    rhs=z_words[h][:].bitcast(FP8X4),
-                    rhs_scale=z_scales[h][:],
-                    start=True,
-                    stop=True,
-                )
-            for t in range(2 * u, 2 * u + 2):
-                nc.scalar.activation(dst[t][:, cols(h)], acc[h, u][:, t % 2, :], ACT.Copy, scale=SIXTEENTH)
+        def score(acc, words, scales, wide, t, piece):
+            nc.tensor.matmul_mx(
+                out=acc[t][:, piece],
+                lhsT=words[:, P * t : P * (t + 1)].bitcast(FP8X4),
+                lhsT_scale=scales[:, P * t : P * (t + 1)],
+                rhs=z_words[:, piece].bitcast(FP8X4),
+                rhs_scale=z_scales[:, piece],
+                start=True,
+                stop=True,
+            )
+            nc.scalar.activation(wide[t][:, piece], acc[t][:, piece], ACT.Copy, scale=SIXTEENTH)
 
         for h in range(2):
-            for u in range(2):
-                score(a_acc, a_words, a_scales, a, h, u)
-        for u in range(2):
-            for h in range(2):
-                score(b_acc, b_words, b_scales, b, h, u)
+            for t in range(PACK):
+                score(a_acc, a_words, a_scales, wide_a, t, cols(h))
+        for t in range(PACK):
+            score(b_acc, b_words, b_scales, wide_b, t, first)
 
         out_rows = out_0.rearrange("(p t) j -> p t j", t=PACK)
         out_words = out_1[0].rearrange("p n t -> p (n t)").bitcast(I32)
         o_scales = sb("o_scales", [P, S], U8)
-        for h in range(2):
-            a_far = sb(f"a_far{h}", [P, PACK, HALF], F32)
-            b_far = sb(f"b_far{h}", [P, PACK, HALF], F32)
-            hi = sb(f"hi{h}", [P, PACK, HALF], F32)
-            lo = sb(f"lo{h}", [P, PACK, HALF], F32)
-            res = sb(f"res{h}", [P, PACK, HALF], F32)
-            for u in range(2):
-                pair = slice(2 * u, 2 * u + 2)
-                for t in range(2 * u, 2 * u + 2):
-                    nc.vector.tensor_copy(a_far[:, t, :], a[t][:].indirect(half_of(n2_l, h)))
-                for t in range(2 * u, 2 * u + 2):
-                    nc.vector.tensor_copy(b_far[:, t, :], b[t][:].indirect(half_of(n3_l, h)))
-                nc.vector.scalar_tensor_tensor(lo[:, pair, :], b_acc[h, u][:], SIXTEENTH, a_far[:, pair, :], ALU.mult, ALU.min)
-                nc.vector.scalar_tensor_tensor(hi[:, pair, :], a_acc[h, u][:], SIXTEENTH, b_far[:, pair, :], ALU.mult, ALU.max)
-            for u in range(2):
-                pair = slice(2 * u, 2 * u + 2)
-                engine = nc.vector if (h, u) == (1, 1) else nc.gpsimd
-                engine.tensor_tensor(res[:, pair, :], hi[:, pair, :], lo[:, pair, :], ALU.subtract)
-                nc.sync.dma_start(out_rows[:, pair, cols(h)], res[:, pair, :])
-            woven = sb(f"o_woven{h}", [P, PACK * HALF], BF16)
-            if h == 0:
-                nc.scalar.copy(*weave(woven, res))
-            else:
-                nc.vector.tensor_copy(*weave(woven, res))
+        o_woven = [sb(f"o_woven{h}", [P, PACK * HALF], BF16) for h in range(2)]
+        res = {(u, h): sb(f"res{u}{h}", [P, 2, HALF], F32) for u in range(2) for h in range(2)}
+        a_far = [sb(f"a_far{t}", [P, S], F32) for t in range(PACK)]
+        b_far = [sb(f"b_far{t}", [P, S], F32) for t in range(PACK)]
+        lo = [sb(f"lo{t}", [P, S], F32) for t in range(PACK)]
+        hi = [sb(f"hi{t}", [P, S], F32) for t in range(PACK)]
+
+        def quantise_out(h):
             o_words = sb(f"o_words{h}", [P, HALF], U32)
-            nc.vector.quantize_mx(out=o_words[:].bitcast(FP8X4), scales=o_scales[:, cols(h)], in_=woven[:])
+            nc.vector.quantize_mx(out=o_words[:].bitcast(FP8X4), scales=o_scales[:, cols(h)], in_=o_woven[h][:])
             nc.sync.dma_start(out_words[:, cols(h)], o_words[:].bitcast(I32))
+
+        for t in range(PACK):
+            u = t // 2
+            pair = slice(2 * u, 2 * u + 2)
+            for piece in pieces(t):
+                nc.vector.tensor_copy(a_far[t][:, piece], wide_a[t][:].indirect(entries(n2_l, piece)))
+                nc.vector.tensor_copy(b_far[t][:, piece], wide_b[t][:].indirect(entries(n3_l, piece)))
+                nc.vector.scalar_tensor_tensor(lo[t][:, piece], b_acc[t][:, piece], SIXTEENTH, a_far[t][:, piece], ALU.mult, ALU.min)
+                nc.vector.scalar_tensor_tensor(hi[t][:, piece], a_acc[t][:, piece], SIXTEENTH, b_far[t][:, piece], ALU.mult, ALU.max)
+                for h in range(piece.start // HALF, piece.stop // HALF):
+                    last = (t, h) == (PACK - 1, 1)
+                    if last:
+                        quantise_out(0)
+                    engine = nc.vector if last else nc.gpsimd
+                    engine.tensor_tensor(res[u, h][:, t % 2, :], hi[t][:, cols(h)], lo[t][:, cols(h)], ALU.subtract)
+                    if t % 2:
+                        nc.sync.dma_start(out_rows[:, pair, cols(h)], res[u, h][:])
+                        copy = nc.vector.tensor_copy if last else nc.scalar.copy
+                        copy(*weave(o_woven[h], res[u, h][:], pair))
+        quantise_out(1)
         for q in range(4):
             queue = nc.sync if q % 2 else nc.scalar
             queue.dma_start(out_2[0, 4 * q : 4 * q + 4, :].bitcast(I32), o_scales[32 * q : 32 * q + 4, :].bitcast(I32))

@@ -149,17 +149,22 @@ def tile_picked_ccmpmaxbtwicp_none_po_kernel(
                 nc.vector.tensor_tensor(big[:, cols(h)], st[:, cols(h)], far[:, cols(h)], ALU.max)
         b_scales = deal_scales("b_scales", b_raw)
 
-        z_planes = [sb(f"z_planes{h}", [P, PACK, HALF], BF16, f"y{h + 2}") for h in range(2)]
         z_woven = [sb(f"z_woven{h}", [P, PACK * HALF], BF16) for h in range(2)]
-        for t in range(PACK):
+        z_early = sb("z_early", [P, 2, S], BF16, "y2")
+        for t in range(2):
+            nc.scalar.activation(z_early[:, t, :], wide_b[t][:, second], ACT.Copy, scale=gain[:, t : t + 1])
+        for h in range(2):
+            nc.scalar.copy(*weave(z_woven[h], z_early[:, :, cols(h)], slice(0, 2)))
+        z_late = [sb(f"z_late{h}", [P, 2, HALF], BF16) for h in range(2)]
+        for t in range(2, PACK):
             for h in range(2):
                 big = wide_b[t][:, second][:, cols(h)]
-                if (t, h) == (PACK - 1, 1):
-                    nc.vector.tensor_scalar(z_planes[h][:, t, :], big, gain[:, t : t + 1], None, ALU.mult)
+                if t == PACK - 1:
+                    nc.vector.tensor_scalar(z_late[h][:, t - 2, :], big, gain[:, t : t + 1], None, ALU.mult)
                 else:
-                    nc.scalar.activation(z_planes[h][:, t, :], big, ACT.Copy, scale=gain[:, t : t + 1])
-        nc.scalar.copy(*weave(z_woven[0], z_planes[0][:], slice(0, PACK)))
-        nc.vector.tensor_copy(*weave(z_woven[1], z_planes[1][:], slice(0, PACK)))
+                    nc.scalar.activation(z_late[h][:, t - 2, :], big, ACT.Copy, scale=gain[:, t : t + 1])
+        for h in range(2):
+            nc.vector.tensor_copy(*weave(z_woven[h], z_late[h][:], slice(2, PACK)))
         z_words = sb("z_words", [P, S], U32)
         z_scales = sb("z_scales", [P, S], U8)
         for h in range(2):
@@ -169,30 +174,30 @@ def tile_picked_ccmpmaxbtwicp_none_po_kernel(
         a_acc = [psum.tile([P, S], F32, name=f"a_acc{t}", tag=f"bank{PACK + t}") for t in range(PACK)]
         b_acc = [psum.tile([P, S], F32, name=f"b_acc{t}", tag=f"bank{t}") for t in range(PACK)]
 
-        def score(acc, words, scales, wide, t, piece):
+        def score(acc, words, scales, wide, t):
             nc.tensor.matmul_mx(
-                out=acc[t][:, piece],
+                out=acc[t][:],
                 lhsT=words[:, P * t : P * (t + 1)].bitcast(FP8X4),
                 lhsT_scale=scales[:, P * t : P * (t + 1)],
-                rhs=z_words[:, piece].bitcast(FP8X4),
-                rhs_scale=z_scales[:, piece],
+                rhs=z_words[:].bitcast(FP8X4),
+                rhs_scale=z_scales[:],
                 start=True,
                 stop=True,
             )
-            nc.scalar.activation(wide[t][:, piece], acc[t][:, piece], ACT.Copy, scale=SIXTEENTH)
+            nc.scalar.activation(wide[t][:, first], acc[t][:], ACT.Copy, scale=SIXTEENTH)
 
-        for h in range(2):
-            for t in range(PACK):
-                score(a_acc, a_words, a_scales, wide_a, t, cols(h))
-        for t in range(PACK):
-            score(b_acc, b_words, b_scales, wide_b, t, first)
+        def score_pair(u):
+            for t in range(2 * u, 2 * u + 2):
+                score(a_acc, a_words, a_scales, wide_a, t)
+            for t in range(2 * u, 2 * u + 2):
+                score(b_acc, b_words, b_scales, wide_b, t)
+
+        score_pair(0)
 
         out_rows = out_0.rearrange("(p t) j -> p t j", t=PACK)
         out_words = out_1[0].rearrange("p n t -> p (n t)").bitcast(I32)
         o_scales = sb("o_scales", [P, S], U8)
         o_woven = [sb(f"o_woven{h}", [P, PACK * HALF], BF16) for h in range(2)]
-        res = {(u, h): sb(f"res{u}{h}", [P, 2, HALF], F32) for u in range(2) for h in range(2)}
-        a_far = [sb(f"a_far{t}", [P, S], F32) for t in range(PACK)]
         b_far = [sb(f"b_far{t}", [P, S], F32) for t in range(PACK)]
         lo = [sb(f"lo{t}", [P, S], F32) for t in range(PACK)]
         hi = [sb(f"hi{t}", [P, S], F32) for t in range(PACK)]
@@ -202,24 +207,54 @@ def tile_picked_ccmpmaxbtwicp_none_po_kernel(
             nc.vector.quantize_mx(out=o_words[:].bitcast(FP8X4), scales=o_scales[:, cols(h)], in_=o_woven[h][:])
             nc.sync.dma_start(out_words[:, cols(h)], o_words[:].bitcast(I32))
 
-        for t in range(PACK):
-            u = t // 2
-            pair = slice(2 * u, 2 * u + 2)
+        def fetch_a(t, piece, tag):
+            a_far = sb(f"a_far{t}_{piece.start}", [P, piece.stop - piece.start], F32, tag)
+            nc.vector.tensor_copy(a_far[:], wide_a[t][:].indirect(entries(n2_l, piece)))
+            return a_far
+
+        def fetch_b(t, piece):
+            nc.vector.tensor_copy(b_far[t][:, piece], wide_b[t][:].indirect(entries(n3_l, piece)))
+
+        def larger(t, piece):
+            nc.vector.scalar_tensor_tensor(hi[t][:, piece], a_acc[t][:, piece], SIXTEENTH, b_far[t][:, piece], ALU.mult, ALU.max)
+
+        res_early = sb("res_early", [P, 2, S], F32)
+        excess = []
+        for t in range(2):
+            a_far = fetch_a(t, first, f"a_far{t}")
+            diff = sb(f"diff{t}", [P, S], F32)
+            nc.gpsimd.tensor_tensor(diff[:], wide_b[t][:, first], a_far[:], ALU.subtract)
+            excess.append(sb(f"excess{t}", [P, S], F32))
+            nc.scalar.activation(excess[t][:], diff[:], ACT.Relu)
+        score_pair(1)
+        for t in range(2):
+            fetch_b(t, first)
+        for t in range(2):
+            larger(t, first)
+            nc.gpsimd.tensor_tensor(lo[t][:], wide_b[t][:, first], excess[t][:], ALU.subtract)
+        for t in range(2):
+            nc.gpsimd.tensor_tensor(res_early[:, t, :], hi[t][:], lo[t][:], ALU.subtract)
+        nc.sync.dma_start(out_rows[:, 0:2, :], res_early[:])
+        for h in range(2):
+            nc.scalar.copy(*weave(o_woven[h], res_early[:, :, cols(h)], slice(0, 2)))
+
+        res_late = [sb(f"res_late{h}", [P, 2, HALF], F32, f"lo{h}") for h in range(2)]
+        for t in range(2, PACK):
             for piece in pieces(t):
-                nc.vector.tensor_copy(a_far[t][:, piece], wide_a[t][:].indirect(entries(n2_l, piece)))
-                nc.vector.tensor_copy(b_far[t][:, piece], wide_b[t][:].indirect(entries(n3_l, piece)))
-                nc.vector.scalar_tensor_tensor(lo[t][:, piece], b_acc[t][:, piece], SIXTEENTH, a_far[t][:, piece], ALU.mult, ALU.min)
-                nc.vector.scalar_tensor_tensor(hi[t][:, piece], a_acc[t][:, piece], SIXTEENTH, b_far[t][:, piece], ALU.mult, ALU.max)
+                a_far = fetch_a(t, piece, "a_far1")
+                fetch_b(t, piece)
+                nc.vector.scalar_tensor_tensor(lo[t][:, piece], b_acc[t][:, piece], SIXTEENTH, a_far[:], ALU.mult, ALU.min)
+                larger(t, piece)
                 for h in range(piece.start // HALF, piece.stop // HALF):
                     last = (t, h) == (PACK - 1, 1)
                     if last:
                         quantise_out(0)
                     engine = nc.vector if last else nc.gpsimd
-                    engine.tensor_tensor(res[u, h][:, t % 2, :], hi[t][:, cols(h)], lo[t][:, cols(h)], ALU.subtract)
-                    if t % 2:
-                        nc.sync.dma_start(out_rows[:, pair, cols(h)], res[u, h][:])
+                    engine.tensor_tensor(res_late[h][:, t - 2, :], hi[t][:, cols(h)], lo[t][:, cols(h)], ALU.subtract)
+                    if t == PACK - 1:
+                        nc.sync.dma_start(out_rows[:, 2:PACK, cols(h)], res_late[h][:])
                         copy = nc.vector.tensor_copy if last else nc.scalar.copy
-                        copy(*weave(o_woven[h], res[u, h][:], pair))
+                        copy(*weave(o_woven[h], res_late[h][:], slice(2, PACK)))
         quantise_out(1)
         for q in range(4):
             queue = nc.sync if q % 2 else nc.scalar

@@ -2,8 +2,9 @@ from contextlib import ExitStack
 
 import concourse.mybir as mybir
 
-K, T, S, H, C = 512, 2048, 512, 512, 512
-FLOPS = 3 * 2 * 512 * 512 * 512
+T = 2048
+S = 512
+FLOPS = 3 * 2 * S * S * S
 
 F32 = mybir.dt.float32
 BF16 = mybir.dt.bfloat16
@@ -17,9 +18,15 @@ ACT = mybir.ActivationFunctionType
 ALU = mybir.AluOpType
 
 P = 128
-PACK = 4
-HALF = 256
-LIST_COLS = HALF // 16
+PLANES = 4
+LAST = PLANES - 1
+EARLY = slice(0, 2)
+LATE = slice(2, 4)
+QUADRANTS = 4
+STRIPE = 16
+HALF = S // 2
+FRONT = slice(0, S)
+BACK = slice(S, 2 * S)
 SIXTEENTH = 0.0625
 
 
@@ -35,40 +42,52 @@ def tile_picked_ccmpmaxbtwicp_none_po_kernel(
             return keep.tile(shape, dtype, name=name, tag=tag or name, align_bytes=64)
 
         def load_list(name, src):
-            lst = keep.tile([P, S // 16], U16, name=name)
+            lst = keep.tile([P, S // STRIPE], U16, name=name)
             nc.sync.dma_start(lst[:], src)
             return lst
 
-        def half_of(lst, h):
-            return lst[:, h * LIST_COLS : (h + 1) * LIST_COLS]
-
-        def cols(h):
+        def half(h):
             return slice(h * HALF, (h + 1) * HALF)
 
+        def entries(lst, piece):
+            return lst[:, piece.start // STRIPE : piece.stop // STRIPE]
+
+        def scale_partitions(tile, q):
+            return tile[32 * q : 32 * q + 4, :].bitcast(I32)
+
+        def scale_rows(dram, q):
+            return dram[0, 4 * q : 4 * q + 4, :].bitcast(I32)
+
+        def weave(woven, pair, planes):
+            return (
+                woven[:].rearrange("p (j t) -> p j t", t=PLANES)[:, :, planes],
+                pair.rearrange("p t j -> p j t"),
+            )
+
         xs = sb("xs", [P, T], U8)
-        ws = sb("ws", [P, H], U8)
+        ws = sb("ws", [P, S], U8)
         warm = sb("warm", [P, 8], F32)
         nc.gpsimd.memset(xs[:].bitcast(I32), 0)
         nc.gpsimd.memset(ws[:].bitcast(I32), 0)
         nc.vector.memset(warm[:, 0:1], 0.0)
         nc.scalar.activation(warm[:, 1:2], warm[:, 0:1], ACT.Sigmoid)
         offs_l = load_list("offs_l", offs)
-        ww = sb("ww", [P, 2 * H], U8)
+        ww = sb("ww", [P, 2 * S], U8)
         nc.sync.dma_start(ww[:].bitcast(I32), w1_words[0].bitcast(I32))
         xw = sb("xw", [P, T], U32)
         x_rows = x_words[0].rearrange("p n t -> p (n t)").bitcast(I32)
         nc.sync.dma_start(xw[:, : T // 2].bitcast(I32), x_rows[:, : T // 2])
-        for q in range(4):
-            nc.sync.dma_start(xs[32 * q : 32 * q + 4, :].bitcast(I32), x_scales[0, 4 * q : 4 * q + 4, :].bitcast(I32))
+        for q in range(QUADRANTS):
+            nc.sync.dma_start(scale_partitions(xs, q), scale_rows(x_scales, q))
         nc.sync.dma_start(xw[:, T // 2 :].bitcast(I32), x_rows[:, T // 2 :])
-        for q in range(4):
-            queue = nc.gpsimd if q >= 2 else nc.sync
-            queue.dma_start(ws[32 * q : 32 * q + 4, :].bitcast(I32), w1_scales[0, 4 * q : 4 * q + 4, :].bitcast(I32))
+        for q in range(QUADRANTS):
+            queue = nc.gpsimd if q >= QUADRANTS // 2 else nc.sync
+            queue.dma_start(scale_partitions(ws, q), scale_rows(w1_scales, q))
         ca_l = load_list("ca_l", ca)
         n1_l = load_list("n1_l", n1)
         cb_l = load_list("cb_l", cb)
-        gain = sb("gain", [P, PACK], F32)
-        nc.sync.dma_start(gain[:], gs.rearrange("(p t) o -> p (t o)", t=PACK))
+        gain = sb("gain", [P, PLANES], F32)
+        nc.sync.dma_start(gain[:], gs.rearrange("(p t) o -> p (t o)", t=PLANES))
         n2_l = load_list("n2_l", n2)
         n3_l = load_list("n3_l", n3)
 
@@ -77,22 +96,22 @@ def tile_picked_ccmpmaxbtwicp_none_po_kernel(
             nc.vector.tensor_copy(picked[:], xs[:].indirect(lst[:]))
             return picked
 
-        def deal_scales(name, src, tag=None):
-            dealt = sb(name, [P, S], U8, tag)
+        def deal_scales(name, src):
+            dealt = sb(name, [P, S], U8)
             nc.vector.tensor_copy(
-                dealt[:].rearrange("p (t m) -> p m t", t=PACK), src[:].rearrange("p (m t) -> p m t", t=PACK)
+                dealt[:].rearrange("p (t m) -> p t m", t=PLANES), src[:].rearrange("p (m t) -> p t m", t=PLANES)
             )
             return dealt
 
-        def pick_words_dealt(name, lst, tag=None):
+        def pick_words_dealt(name, lst, tag):
             dealt = sb(name, [P, S], U32, tag)
-            nc.vector.tensor_copy(dealt[:].rearrange("p (t m) -> p m t", t=PACK), xw[:].indirect(lst[:]))
+            nc.vector.tensor_copy(dealt[:].rearrange("p (t m) -> p m t", t=PLANES), xw[:].indirect(lst[:]))
             return dealt
 
-        w_words = sb("w_words", [P, 2 * H], U8)
+        w_words = sb("w_words", [P, 2 * S], U8)
         nc.vector.tensor_copy(
-            w_words[:].rearrange("p (t m b) -> p m t b", t=PACK, b=2),
-            ww[:].rearrange("p (m t b) -> p m t b", t=PACK, b=2),
+            w_words[:].rearrange("p (t m b) -> p t m b", t=PLANES, b=2),
+            ww[:].rearrange("p (m t b) -> p t m b", t=PLANES, b=2),
         )
         q_scales = pick_scales("q_scales", offs_l)
         q_words = sb("q_words", [P, S], U32)
@@ -103,15 +122,13 @@ def tile_picked_ccmpmaxbtwicp_none_po_kernel(
         a_words = pick_words_dealt("a_words", ca_l, "ww")
         b_raw = pick_scales("b_raw", cb_l, "ws")
 
-        first = slice(0, S)
-        second = slice(S, 2 * S)
         y = []
-        wide_a = [sb(f"wide_a{t}", [P, 2 * S], F32) for t in range(PACK)]
-        wide_b = [sb(f"wide_b{t}", [P, 2 * S], F32) for t in range(PACK)]
-        for t in range(PACK):
-            acc = psum.tile([P, S], F32, name=f"y_acc{t}", tag=f"bank{t}")
+        wide_a = [sb(f"wide_a{t}", [P, 2 * S], F32) for t in range(PLANES)]
+        wide_b = [sb(f"wide_b{t}", [P, 2 * S], F32) for t in range(PLANES)]
+        for t in range(PLANES):
+            y_acc = psum.tile([P, S], F32, name=f"y_acc{t}", tag=f"bank{t}")
             nc.tensor.matmul_mx(
-                out=acc[:],
+                out=y_acc[:],
                 lhsT=w_words[:, 2 * P * t : 2 * P * (t + 1)].bitcast(FP4X4),
                 lhsT_scale=w_scales[:, P * t : P * (t + 1)],
                 rhs=q_words[:].bitcast(FP8X4),
@@ -120,59 +137,46 @@ def tile_picked_ccmpmaxbtwicp_none_po_kernel(
                 stop=True,
             )
             y.append(sb(f"y{t}", [P, S], F32))
-            nc.scalar.copy(y[t][:], acc[:])
+            nc.scalar.copy(y[t][:], y_acc[:])
             for h in range(2):
-                nc.scalar.activation(wide_a[t][:, second][:, cols(h)], y[t][:].indirect(half_of(n1_l, h)), ACT.Sigmoid)
+                nc.scalar.activation(wide_a[t][:, BACK][:, half(h)], y[t][:].indirect(entries(n1_l, half(h))), ACT.Sigmoid)
 
-        def pieces(t):
-            if t < PACK - 1:
-                return [slice(0, S)]
-            return [cols(0), cols(1)]
-
-        def entries(lst, piece):
-            return lst[:, piece.start // 16 : piece.stop // 16]
-
-        def weave(dst, src, planes):
-            return (
-                dst[:].rearrange("p (c i t) -> p c t i", i=4, t=PACK)[:, :, planes, :],
-                src.rearrange("p t (c i) -> p c t i", i=4),
-            )
-
-        for t in range(PACK):
-            st = wide_a[t][:, first]
-            far = wide_a[(t + 2) % PACK][:, first]
-            big = wide_b[t][:, second]
-            nc.gpsimd.tensor_tensor(st, y[t][:], wide_a[t][:, second], ALU.mult)
+        for t in range(PLANES):
+            st = wide_a[t][:, FRONT]
+            st_far = wide_a[(t + 2) % PLANES][:, FRONT]
+            st_max = wide_b[t][:, BACK]
+            nc.gpsimd.tensor_tensor(st, y[t][:], wide_a[t][:, BACK], ALU.mult)
             for h in range(2):
-                nc.vector.tensor_copy(far[:, cols(h)], wide_a[t][:].indirect(half_of(n1_l, h)))
+                nc.vector.tensor_copy(st_far[:, half(h)], wide_a[t][:].indirect(entries(n1_l, half(h))))
             for h in range(2):
-                nc.vector.tensor_tensor(big[:, cols(h)], st[:, cols(h)], far[:, cols(h)], ALU.max)
+                nc.vector.tensor_tensor(st_max[:, half(h)], st[:, half(h)], st_far[:, half(h)], ALU.max)
         b_scales = deal_scales("b_scales", b_raw)
 
-        z_woven = [sb(f"z_woven{h}", [P, PACK * HALF], BF16) for h in range(2)]
+        z_woven = [sb(f"z_woven{h}", [P, PLANES * HALF], BF16) for h in range(2)]
         z_early = sb("z_early", [P, 2, S], BF16, "y2")
-        for t in range(2):
-            nc.scalar.activation(z_early[:, t, :], wide_b[t][:, second], ACT.Copy, scale=gain[:, t : t + 1])
+        for t in range(EARLY.start, EARLY.stop):
+            nc.scalar.activation(z_early[:, t, :], wide_b[t][:, BACK], ACT.Copy, scale=gain[:, t : t + 1])
         for h in range(2):
-            nc.scalar.copy(*weave(z_woven[h], z_early[:, :, cols(h)], slice(0, 2)))
+            nc.scalar.copy(*weave(z_woven[h], z_early[:, :, half(h)], EARLY))
         z_late = [sb(f"z_late{h}", [P, 2, HALF], BF16) for h in range(2)]
-        for t in range(2, PACK):
+        for t in range(LATE.start, LATE.stop):
             for h in range(2):
-                big = wide_b[t][:, second][:, cols(h)]
-                if t == PACK - 1:
-                    nc.vector.tensor_scalar(z_late[h][:, t - 2, :], big, gain[:, t : t + 1], None, ALU.mult)
+                st_max_half = wide_b[t][:, BACK][:, half(h)]
+                z_half = z_late[h][:, t - LATE.start, :]
+                if t == LAST:
+                    nc.vector.tensor_scalar(z_half, st_max_half, gain[:, t : t + 1], None, ALU.mult)
                 else:
-                    nc.scalar.activation(z_late[h][:, t - 2, :], big, ACT.Copy, scale=gain[:, t : t + 1])
+                    nc.scalar.activation(z_half, st_max_half, ACT.Copy, scale=gain[:, t : t + 1])
         for h in range(2):
-            nc.vector.tensor_copy(*weave(z_woven[h], z_late[h][:], slice(2, PACK)))
+            nc.vector.tensor_copy(*weave(z_woven[h], z_late[h][:], LATE))
         z_words = sb("z_words", [P, S], U32)
         z_scales = sb("z_scales", [P, S], U8)
         for h in range(2):
-            nc.vector.quantize_mx(out=z_words[:, cols(h)].bitcast(FP8X4), scales=z_scales[:, cols(h)], in_=z_woven[h][:])
+            nc.vector.quantize_mx(out=z_words[:, half(h)].bitcast(FP8X4), scales=z_scales[:, half(h)], in_=z_woven[h][:])
         b_words = pick_words_dealt("b_words", cb_l, "z_woven1")
 
-        a_acc = [psum.tile([P, S], F32, name=f"a_acc{t}", tag=f"bank{PACK + t}") for t in range(PACK)]
-        b_acc = [psum.tile([P, S], F32, name=f"b_acc{t}", tag=f"bank{t}") for t in range(PACK)]
+        a_acc = [psum.tile([P, S], F32, name=f"a_acc{t}", tag=f"bank{PLANES + t}") for t in range(PLANES)]
+        b_acc = [psum.tile([P, S], F32, name=f"b_acc{t}", tag=f"bank{t}") for t in range(PLANES)]
 
         def score(acc, words, scales, wide, t):
             nc.tensor.matmul_mx(
@@ -184,28 +188,28 @@ def tile_picked_ccmpmaxbtwicp_none_po_kernel(
                 start=True,
                 stop=True,
             )
-            nc.scalar.activation(wide[t][:, first], acc[t][:], ACT.Copy, scale=SIXTEENTH)
+            nc.scalar.activation(wide[t][:, FRONT], acc[t][:], ACT.Copy, scale=SIXTEENTH)
 
-        def score_pair(u):
-            for t in range(2 * u, 2 * u + 2):
+        def score_pair(planes):
+            for t in range(planes.start, planes.stop):
                 score(a_acc, a_words, a_scales, wide_a, t)
-            for t in range(2 * u, 2 * u + 2):
+            for t in range(planes.start, planes.stop):
                 score(b_acc, b_words, b_scales, wide_b, t)
 
-        score_pair(0)
+        score_pair(EARLY)
 
-        out_rows = out_0.rearrange("(p t) j -> p t j", t=PACK)
+        out_rows = out_0.rearrange("(p t) j -> p t j", t=PLANES)
         out_words = out_1[0].rearrange("p n t -> p (n t)").bitcast(I32)
         o_scales = sb("o_scales", [P, S], U8)
-        o_woven = [sb(f"o_woven{h}", [P, PACK * HALF], BF16) for h in range(2)]
-        b_far = [sb(f"b_far{t}", [P, S], F32) for t in range(PACK)]
-        lo = [sb(f"lo{t}", [P, S], F32) for t in range(PACK)]
-        hi = [sb(f"hi{t}", [P, S], F32) for t in range(PACK)]
+        o_woven = [sb(f"o_woven{h}", [P, PLANES * HALF], BF16) for h in range(2)]
+        b_far = [sb(f"b_far{t}", [P, S], F32) for t in range(PLANES)]
+        lo = [sb(f"lo{t}", [P, S], F32) for t in range(PLANES)]
+        hi = [sb(f"hi{t}", [P, S], F32) for t in range(PLANES)]
 
         def quantise_out(h):
             o_words = sb(f"o_words{h}", [P, HALF], U32)
-            nc.vector.quantize_mx(out=o_words[:].bitcast(FP8X4), scales=o_scales[:, cols(h)], in_=o_woven[h][:])
-            nc.sync.dma_start(out_words[:, cols(h)], o_words[:].bitcast(I32))
+            nc.vector.quantize_mx(out=o_words[:].bitcast(FP8X4), scales=o_scales[:, half(h)], in_=o_woven[h][:])
+            nc.sync.dma_start(out_words[:, half(h)], o_words[:].bitcast(I32))
 
         def fetch_a(t, piece, tag):
             a_far = sb(f"a_far{t}_{piece.start}", [P, piece.stop - piece.start], F32, tag)
@@ -215,47 +219,47 @@ def tile_picked_ccmpmaxbtwicp_none_po_kernel(
         def fetch_b(t, piece):
             nc.vector.tensor_copy(b_far[t][:, piece], wide_b[t][:].indirect(entries(n3_l, piece)))
 
-        def larger(t, piece):
+        def make_hi(t, piece):
             nc.vector.scalar_tensor_tensor(hi[t][:, piece], a_acc[t][:, piece], SIXTEENTH, b_far[t][:, piece], ALU.mult, ALU.max)
 
         res_early = sb("res_early", [P, 2, S], F32)
         excess = []
-        for t in range(2):
-            a_far = fetch_a(t, first, f"a_far{t}")
+        for t in range(EARLY.start, EARLY.stop):
+            a_far = fetch_a(t, FRONT, f"a_far{t}")
             diff = sb(f"diff{t}", [P, S], F32)
-            nc.gpsimd.tensor_tensor(diff[:], wide_b[t][:, first], a_far[:], ALU.subtract)
+            nc.gpsimd.tensor_tensor(diff[:], wide_b[t][:, FRONT], a_far[:], ALU.subtract)
             excess.append(sb(f"excess{t}", [P, S], F32))
             nc.scalar.activation(excess[t][:], diff[:], ACT.Relu)
-        score_pair(1)
-        for t in range(2):
-            fetch_b(t, first)
-        for t in range(2):
-            larger(t, first)
-            nc.gpsimd.tensor_tensor(lo[t][:], wide_b[t][:, first], excess[t][:], ALU.subtract)
-        for t in range(2):
+        score_pair(LATE)
+        for t in range(EARLY.start, EARLY.stop):
+            fetch_b(t, FRONT)
+        for t in range(EARLY.start, EARLY.stop):
+            make_hi(t, FRONT)
+            nc.gpsimd.tensor_tensor(lo[t][:], wide_b[t][:, FRONT], excess[t][:], ALU.subtract)
+        for t in range(EARLY.start, EARLY.stop):
             nc.gpsimd.tensor_tensor(res_early[:, t, :], hi[t][:], lo[t][:], ALU.subtract)
-        nc.sync.dma_start(out_rows[:, 0:2, :], res_early[:])
+        nc.sync.dma_start(out_rows[:, EARLY, :], res_early[:])
         for h in range(2):
-            nc.scalar.copy(*weave(o_woven[h], res_early[:, :, cols(h)], slice(0, 2)))
+            nc.scalar.copy(*weave(o_woven[h], res_early[:, :, half(h)], EARLY))
 
         res_late = [sb(f"res_late{h}", [P, 2, HALF], F32, f"lo{h}") for h in range(2)]
-        for t in range(2, PACK):
-            for piece in pieces(t):
+        for t in range(LATE.start, LATE.stop):
+            for piece in [half(0), half(1)] if t == LAST else [FRONT]:
                 a_far = fetch_a(t, piece, "a_far1")
                 fetch_b(t, piece)
                 nc.vector.scalar_tensor_tensor(lo[t][:, piece], b_acc[t][:, piece], SIXTEENTH, a_far[:], ALU.mult, ALU.min)
-                larger(t, piece)
+                make_hi(t, piece)
                 for h in range(piece.start // HALF, piece.stop // HALF):
-                    last = (t, h) == (PACK - 1, 1)
-                    if last:
+                    at_end = (t, h) == (LAST, 1)
+                    if at_end:
                         quantise_out(0)
-                    engine = nc.vector if last else nc.gpsimd
-                    engine.tensor_tensor(res_late[h][:, t - 2, :], hi[t][:, cols(h)], lo[t][:, cols(h)], ALU.subtract)
-                    if t == PACK - 1:
-                        nc.sync.dma_start(out_rows[:, 2:PACK, cols(h)], res_late[h][:])
-                        copy = nc.vector.tensor_copy if last else nc.scalar.copy
-                        copy(*weave(o_woven[h], res_late[h][:], slice(2, PACK)))
+                    engine = nc.vector if at_end else nc.gpsimd
+                    engine.tensor_tensor(res_late[h][:, t - LATE.start, :], hi[t][:, half(h)], lo[t][:, half(h)], ALU.subtract)
+                    if t == LAST:
+                        nc.sync.dma_start(out_rows[:, LATE, half(h)], res_late[h][:])
+                        copy = nc.vector.tensor_copy if at_end else nc.scalar.copy
+                        copy(*weave(o_woven[h], res_late[h][:], LATE))
         quantise_out(1)
-        for q in range(4):
+        for q in range(QUADRANTS):
             queue = nc.sync if q % 2 else nc.scalar
-            queue.dma_start(out_2[0, 4 * q : 4 * q + 4, :].bitcast(I32), o_scales[32 * q : 32 * q + 4, :].bitcast(I32))
+            queue.dma_start(scale_rows(out_2, q), scale_partitions(o_scales, q))

from contextlib import ExitStack

import concourse.mybir as mybir

T = 2048
S = 512
FLOPS = 3 * 2 * S * S * S

F32 = mybir.dt.float32
BF16 = mybir.dt.bfloat16
I32 = mybir.dt.int32
U32 = mybir.dt.uint32
U16 = mybir.dt.uint16
U8 = mybir.dt.uint8
FP8X4 = mybir.dt.float8_e4m3fn_x4
FP4X4 = mybir.dt.float4_e2m1fn_x4
ACT = mybir.ActivationFunctionType
ALU = mybir.AluOpType

P = 128
PLANES = 4
LAST = PLANES - 1
EARLY = slice(0, 2)
LATE = slice(2, 4)
QUADRANTS = 4
STRIPE = 16
HALF = S // 2
FRONT = slice(0, S)
BACK = slice(S, 2 * S)
SIXTEENTH = 0.0625


def tile_picked_ccmpmaxbtwicp_none_po_kernel(
    tc, x_words, x_scales, w1_words, w1_scales, gs, offs, n1, ca, cb, n2, n3, out_0, out_1, out_2
):
    nc = tc.nc
    with ExitStack() as ctx:
        keep = ctx.enter_context(tc.tile_pool(name="keep", bufs=1))
        psum = ctx.enter_context(tc.psum_pool(name="psum", bufs=1))

        def sb(name, shape, dtype, tag=None):
            return keep.tile(shape, dtype, name=name, tag=tag or name, align_bytes=64)

        def load_list(name, src):
            lst = keep.tile([P, S // STRIPE], U16, name=name)
            nc.sync.dma_start(lst[:], src)
            return lst

        def half(h):
            return slice(h * HALF, (h + 1) * HALF)

        def entries(lst, piece):
            return lst[:, piece.start // STRIPE : piece.stop // STRIPE]

        def scale_partitions(tile, q):
            return tile[32 * q : 32 * q + 4, :].bitcast(I32)

        def scale_rows(dram, q):
            return dram[0, 4 * q : 4 * q + 4, :].bitcast(I32)

        def weave(woven, pair, planes):
            return (
                woven[:].rearrange("p (j t) -> p j t", t=PLANES)[:, :, planes],
                pair.rearrange("p t j -> p j t"),
            )

        xs = sb("xs", [P, T], U8)
        ws = sb("ws", [P, S], U8)
        warm = sb("warm", [P, 8], F32)
        nc.gpsimd.memset(xs[:].bitcast(I32), 0)
        nc.gpsimd.memset(ws[:].bitcast(I32), 0)
        nc.vector.memset(warm[:, 0:1], 0.0)
        nc.scalar.activation(warm[:, 1:2], warm[:, 0:1], ACT.Sigmoid)
        offs_l = load_list("offs_l", offs)
        ww = sb("ww", [P, 2 * S], U8)
        nc.sync.dma_start(ww[:].bitcast(I32), w1_words[0].bitcast(I32))
        xw = sb("xw", [P, T], U32)
        x_rows = x_words[0].rearrange("p n t -> p (n t)").bitcast(I32)
        nc.sync.dma_start(xw[:, : T // 2].bitcast(I32), x_rows[:, : T // 2])
        for q in range(QUADRANTS):
            nc.sync.dma_start(scale_partitions(xs, q), scale_rows(x_scales, q))
        nc.sync.dma_start(xw[:, T // 2 :].bitcast(I32), x_rows[:, T // 2 :])
        for q in range(QUADRANTS):
            queue = nc.gpsimd if q >= QUADRANTS // 2 else nc.sync
            queue.dma_start(scale_partitions(ws, q), scale_rows(w1_scales, q))
        ca_l = load_list("ca_l", ca)
        n1_l = load_list("n1_l", n1)
        cb_l = load_list("cb_l", cb)
        gain = sb("gain", [P, PLANES], F32)
        nc.sync.dma_start(gain[:], gs.rearrange("(p t) o -> p (t o)", t=PLANES))
        n2_l = load_list("n2_l", n2)
        n3_l = load_list("n3_l", n3)

        def pick_scales(name, lst, tag=None):
            picked = sb(name, [P, S], U8, tag)
            nc.vector.tensor_copy(picked[:], xs[:].indirect(lst[:]))
            return picked

        def deal_scales(name, src):
            dealt = sb(name, [P, S], U8)
            nc.vector.tensor_copy(
                dealt[:].rearrange("p (t m) -> p t m", t=PLANES), src[:].rearrange("p (m t) -> p t m", t=PLANES)
            )
            return dealt

        def pick_words_dealt(name, lst, tag):
            dealt = sb(name, [P, S], U32, tag)
            nc.vector.tensor_copy(dealt[:].rearrange("p (t m) -> p m t", t=PLANES), xw[:].indirect(lst[:]))
            return dealt

        w_words = sb("w_words", [P, 2 * S], U8)
        nc.vector.tensor_copy(
            w_words[:].rearrange("p (t m b) -> p t m b", t=PLANES, b=2),
            ww[:].rearrange("p (m t b) -> p t m b", t=PLANES, b=2),
        )
        q_scales = pick_scales("q_scales", offs_l)
        q_words = sb("q_words", [P, S], U32)
        nc.vector.tensor_copy(q_words[:], xw[:].indirect(offs_l[:]))
        w_scales = deal_scales("w_scales", ws)

        a_scales = deal_scales("a_scales", pick_scales("a_raw", ca_l, "ws"))
        a_words = pick_words_dealt("a_words", ca_l, "ww")
        b_raw = pick_scales("b_raw", cb_l, "ws")

        y = []
        wide_a = [sb(f"wide_a{t}", [P, 2 * S], F32) for t in range(PLANES)]
        wide_b = [sb(f"wide_b{t}", [P, 2 * S], F32) for t in range(PLANES)]
        for t in range(PLANES):
            y_acc = psum.tile([P, S], F32, name=f"y_acc{t}", tag=f"bank{t}")
            nc.tensor.matmul_mx(
                out=y_acc[:],
                lhsT=w_words[:, 2 * P * t : 2 * P * (t + 1)].bitcast(FP4X4),
                lhsT_scale=w_scales[:, P * t : P * (t + 1)],
                rhs=q_words[:].bitcast(FP8X4),
                rhs_scale=q_scales[:],
                start=True,
                stop=True,
            )
            y.append(sb(f"y{t}", [P, S], F32))
            nc.scalar.copy(y[t][:], y_acc[:])
            for h in range(2):
                nc.scalar.activation(wide_a[t][:, BACK][:, half(h)], y[t][:].indirect(entries(n1_l, half(h))), ACT.Sigmoid)

        for t in range(PLANES):
            st = wide_a[t][:, FRONT]
            st_far = wide_a[(t + 2) % PLANES][:, FRONT]
            st_max = wide_b[t][:, BACK]
            nc.gpsimd.tensor_tensor(st, y[t][:], wide_a[t][:, BACK], ALU.mult)
            for h in range(2):
                nc.vector.tensor_copy(st_far[:, half(h)], wide_a[t][:].indirect(entries(n1_l, half(h))))
            for h in range(2):
                nc.vector.tensor_tensor(st_max[:, half(h)], st[:, half(h)], st_far[:, half(h)], ALU.max)
        b_scales = deal_scales("b_scales", b_raw)

        z_woven = [sb(f"z_woven{h}", [P, PLANES * HALF], BF16) for h in range(2)]
        z_early = sb("z_early", [P, 2, S], BF16, "y2")
        for t in range(EARLY.start, EARLY.stop):
            nc.scalar.activation(z_early[:, t, :], wide_b[t][:, BACK], ACT.Copy, scale=gain[:, t : t + 1])
        for h in range(2):
            nc.scalar.copy(*weave(z_woven[h], z_early[:, :, half(h)], EARLY))
        z_late = [sb(f"z_late{h}", [P, 2, HALF], BF16) for h in range(2)]
        for t in range(LATE.start, LATE.stop):
            for h in range(2):
                st_max_half = wide_b[t][:, BACK][:, half(h)]
                z_half = z_late[h][:, t - LATE.start, :]
                if t == LAST:
                    nc.vector.tensor_scalar(z_half, st_max_half, gain[:, t : t + 1], None, ALU.mult)
                else:
                    nc.scalar.activation(z_half, st_max_half, ACT.Copy, scale=gain[:, t : t + 1])
        for h in range(2):
            nc.vector.tensor_copy(*weave(z_woven[h], z_late[h][:], LATE))
        z_words = sb("z_words", [P, S], U32)
        z_scales = sb("z_scales", [P, S], U8)
        for h in range(2):
            nc.vector.quantize_mx(out=z_words[:, half(h)].bitcast(FP8X4), scales=z_scales[:, half(h)], in_=z_woven[h][:])
        b_words = pick_words_dealt("b_words", cb_l, "z_woven1")

        a_acc = [psum.tile([P, S], F32, name=f"a_acc{t}", tag=f"bank{PLANES + t}") for t in range(PLANES)]
        b_acc = [psum.tile([P, S], F32, name=f"b_acc{t}", tag=f"bank{t}") for t in range(PLANES)]

        def score(acc, words, scales, wide, t):
            nc.tensor.matmul_mx(
                out=acc[t][:],
                lhsT=words[:, P * t : P * (t + 1)].bitcast(FP8X4),
                lhsT_scale=scales[:, P * t : P * (t + 1)],
                rhs=z_words[:].bitcast(FP8X4),
                rhs_scale=z_scales[:],
                start=True,
                stop=True,
            )
            nc.scalar.activation(wide[t][:, FRONT], acc[t][:], ACT.Copy, scale=SIXTEENTH)

        def score_pair(planes):
            for t in range(planes.start, planes.stop):
                score(a_acc, a_words, a_scales, wide_a, t)
            for t in range(planes.start, planes.stop):
                score(b_acc, b_words, b_scales, wide_b, t)

        score_pair(EARLY)

        out_rows = out_0.rearrange("(p t) j -> p t j", t=PLANES)
        out_words = out_1[0].rearrange("p n t -> p (n t)").bitcast(I32)
        o_scales = sb("o_scales", [P, S], U8)
        o_woven = [sb(f"o_woven{h}", [P, PLANES * HALF], BF16) for h in range(2)]
        b_far = [sb(f"b_far{t}", [P, S], F32) for t in range(PLANES)]
        lo = [sb(f"lo{t}", [P, S], F32) for t in range(PLANES)]
        hi = [sb(f"hi{t}", [P, S], F32) for t in range(PLANES)]

        def quantise_out(h):
            o_words = sb(f"o_words{h}", [P, HALF], U32)
            nc.vector.quantize_mx(out=o_words[:].bitcast(FP8X4), scales=o_scales[:, half(h)], in_=o_woven[h][:])
            nc.sync.dma_start(out_words[:, half(h)], o_words[:].bitcast(I32))

        def fetch_a(t, piece, tag):
            a_far = sb(f"a_far{t}_{piece.start}", [P, piece.stop - piece.start], F32, tag)
            nc.vector.tensor_copy(a_far[:], wide_a[t][:].indirect(entries(n2_l, piece)))
            return a_far

        def fetch_b(t, piece):
            nc.vector.tensor_copy(b_far[t][:, piece], wide_b[t][:].indirect(entries(n3_l, piece)))

        def make_hi(t, piece):
            nc.vector.scalar_tensor_tensor(hi[t][:, piece], a_acc[t][:, piece], SIXTEENTH, b_far[t][:, piece], ALU.mult, ALU.max)

        res_early = sb("res_early", [P, 2, S], F32)
        excess = []
        for t in range(EARLY.start, EARLY.stop):
            a_far = fetch_a(t, FRONT, f"a_far{t}")
            diff = sb(f"diff{t}", [P, S], F32)
            nc.gpsimd.tensor_tensor(diff[:], wide_b[t][:, FRONT], a_far[:], ALU.subtract)
            excess.append(sb(f"excess{t}", [P, S], F32))
            nc.scalar.activation(excess[t][:], diff[:], ACT.Relu)
        score_pair(LATE)
        for t in range(EARLY.start, EARLY.stop):
            fetch_b(t, FRONT)
        for t in range(EARLY.start, EARLY.stop):
            make_hi(t, FRONT)
            nc.gpsimd.tensor_tensor(lo[t][:], wide_b[t][:, FRONT], excess[t][:], ALU.subtract)
        for t in range(EARLY.start, EARLY.stop):
            nc.gpsimd.tensor_tensor(res_early[:, t, :], hi[t][:], lo[t][:], ALU.subtract)
        nc.sync.dma_start(out_rows[:, EARLY, :], res_early[:])
        for h in range(2):
            nc.scalar.copy(*weave(o_woven[h], res_early[:, :, half(h)], EARLY))

        res_late = [sb(f"res_late{h}", [P, 2, HALF], F32, f"lo{h}") for h in range(2)]
        for t in range(LATE.start, LATE.stop):
            for piece in [half(0), half(1)] if t == LAST else [FRONT]:
                a_far = fetch_a(t, piece, "a_far1")
                fetch_b(t, piece)
                nc.vector.scalar_tensor_tensor(lo[t][:, piece], b_acc[t][:, piece], SIXTEENTH, a_far[:], ALU.mult, ALU.min)
                make_hi(t, piece)
                for h in range(piece.start // HALF, piece.stop // HALF):
                    at_end = (t, h) == (LAST, 1)
                    if at_end:
                        quantise_out(0)
                    engine = nc.vector if at_end else nc.gpsimd
                    engine.tensor_tensor(res_late[h][:, t - LATE.start, :], hi[t][:, half(h)], lo[t][:, half(h)], ALU.subtract)
                    if t == LAST:
                        nc.sync.dma_start(out_rows[:, LATE, half(h)], res_late[h][:])
                        copy = nc.vector.tensor_copy if at_end else nc.scalar.copy
                        copy(*weave(o_woven[h], res_late[h][:], LATE))
        quantise_out(1)
        for q in range(QUADRANTS):
            queue = nc.sync if q % 2 else nc.scalar
            queue.dma_start(scale_rows(out_2, q), scale_partitions(o_scales, q))
